import numpy as np, ml_dtypes
CORES = [2,3,42,43,82,83,122,123]
N = 8
import mx_ref
BF = ml_dtypes.bfloat16
def entries(a):
    return np.ascontiguousarray(a.T).reshape(-1)
def table(e):
    return np.ascontiguousarray(np.reshape(e, (-1, 16)).T).astype(np.int32)
def gentries(a):
    return np.ascontiguousarray(a.reshape(8, 16, -1).transpose(0, 2, 1)).reshape(8, -1)
def gtable(e):
    e = np.asarray(e); return np.ascontiguousarray(e.reshape(8, -1, 16).transpose(0, 2, 1)).reshape(128, -1).astype(np.int32)
def cols(t, e):
    v = np.concatenate([t.reshape(128, -1, 4), np.zeros((128, 1, 4), BF)], axis=1)
    return np.ascontiguousarray(v[:, e]).reshape(128, -1)
def gpick(z, e):
    return np.concatenate([z[16 * g:16 * g + 16][:, e[g]] for g in range(8)])
def tile(rs):
    return np.stack(rs, axis=2).reshape(128, -1).astype(BF)
def cut(t, i, w=512):
    return t[:, w * i:w * i + w]
def f(rng, *shape):
    return mx_ref.flush((rng.standard_normal(shape, dtype=np.float32) * np.exp2(rng.integers(-2, 3, shape[:-1] + (1,)))).astype(BF))
def wide(rng, *shape, cols=0):
    v = rng.standard_normal(shape, dtype=np.float32) * np.exp2(rng.integers(-12, 13, shape)).astype(np.float32)
    if cols: v *= np.repeat(np.exp2(rng.integers(-cols, cols + 1, shape[:-2] + (1, shape[-1] // 4))) * (rng.random(shape[:-2] + (1, shape[-1] // 4)) > 0.0625), 4, axis=-1).astype(np.float32)
    return mx_ref.flush(v.astype(BF))
T, CAPP, KH, O = 512, 64, 512, 1
def lists(rng, kind="plain"):
    g = np.full((N, N * CAPP), -1)
    for s in range(N):
        for d in range(N):
            if d == s: continue
            n = rng.integers(0, CAPP + 1)
            if kind in ("foreign", "one"): n = CAPP
            if kind == "own": n = CAPP if d == (s + 1) % N else 0
            g[s, d * CAPP + rng.permutation(CAPP)[:n]] = rng.permutation(T)[:n] if n == CAPP else rng.integers(0, T, n)
    p = []
    for r in range(N):
        near = np.arange(T)
        far = T + np.flatnonzero(g[:, r * CAPP:(r + 1) * CAPP].reshape(-1) >= 0)
        if len(far) == 0: far = near
        e = np.where(rng.random((8, KH)) < 0.5, rng.choice(near, (8, KH)), rng.choice(far, (8, KH)))
        if kind == "agree": e = np.repeat(e[:1], 8, axis=0)
        if kind == "foreign": e = rng.choice(far, (8, KH))
        if kind == "own": e = rng.choice(near, (8, KH))
        if kind == "one":
            k = rng.permutation(np.concatenate([rng.permutation(near)[:4], rng.permutation(far)[:4]]))
            e = np.repeat(k[:, None], KH, axis=1)
        p.append(gtable(e))
    return {"snd": np.stack([table(g[s]) for s in range(N)]), "pk": np.stack(p)}
def setup_inputs(rng):
    return {"x": f(rng, N, 128, 4 * T), "w": f(rng, N, 128, 2048), "v": f(rng, N, 128, O * 512), **lists(rng)}
def setup_inputs_agree(rng):
    return {**setup_inputs(rng), **lists(rng, "agree")}
def setup_inputs_foreign(rng):
    return {**setup_inputs(rng), **lists(rng, "foreign")}
def setup_inputs_own(rng):
    return {**setup_inputs(rng), **lists(rng, "own")}
def setup_inputs_one(rng):
    return {**setup_inputs(rng), **lists(rng, "one")}
def setup_inputs_spread(rng):
    d = setup_inputs(rng); d["x"] = wide(rng, N, 128, 4 * T, cols=8); return d
def check_inputs(d):
    b = []
    g = np.stack([entries(d["snd"][s]) for s in range(N)])
    for r in range(N):
        if g[r].min() < -1 or g[r].max() >= T or (g[r, r * CAPP:(r + 1) * CAPP] != -1).any(): b.append("snd")
        e = gentries(d["pk"][r])
        if e.min() < 0 or e.max() >= T + N * CAPP: b.append("pk")
        else:
            used = g[:, r * CAPP:(r + 1) * CAPP].reshape(-1) >= 0
            if not used[e[e >= T] - T].all(): b.append("pk")
    return b
def reference(x, w, v, snd, pk):
    y = np.zeros((N, 128, O * KH), np.float32)
    for r in range(N):
        t = np.concatenate([x[r]] + [cols(x[s], entries(snd[s])[r * CAPP:(r + 1) * CAPP]) for s in range(N)], axis=1)
        q = mx_ref.quantize(np.ascontiguousarray(t))
        e = gentries(pk[r])
        rs = []
        for b in range(4):
            z = mx_ref.matmul(mx_ref.quantize(np.ascontiguousarray(cut(w[r], b))), q)
            rs.append(np.maximum(gpick(z, e), np.float32(0)) * np.float32(0.05))
        h = mx_ref.quantize(np.ascontiguousarray(tile(rs)))
        for o in range(O): y[r][:, KH * o:KH * o + KH] = mx_ref.matmul(mx_ref.quantize(np.ascontiguousarray(cut(v[r], o))), h)
    return {"y": y}

@@ -1,0 +1,237 @@
+from concourse.bass import DstId, RemoteDMATransfer
+from concourse.mybir import dt, AluOpType, ActivationFunctionType
+
+N, W, CAP, PICKS = 8, 512, 64, 512
+PAD = 16
+BS = (0, 2, 1, 3)
+CODES, BYTE = "float8_e4m3fn_x4", "uint8"
+SCRATCH = {
+    "lst": ("sbuf", [128, 32], "int32"),
+    "pkl": ("sbuf", [128, 32], "int32"),
+    "pko": ("sbuf", [128, 32], "uint16"),
+    "xs": ("sbuf", [128, PAD + 4 * W], "bfloat16"),
+    "ws": ("sbuf", [128, 2048], "bfloat16"),
+    "vs": ("sbuf", [128, 512], "bfloat16"),
+    "gath": ("sbuf", [128, 4 * 7 * CAP], "bfloat16"),
+    "sq": ("sbuf", [128, 7 * CAP], CODES),
+    "sp": ("sbuf", [128, 7 * CAP], BYTE),
+    "cq": ("sbuf", [128, W + 7 * CAP], CODES),
+    "cp": ("sbuf", [128, W + 7 * CAP], BYTE),
+    "wq": ("sbuf", [128, 512], CODES),
+    "wp": ("sbuf", [128, 512], BYTE),
+    "vq": ("sbuf", [128, 128], CODES),
+    "vp": ("sbuf", [128, 128], BYTE),
+    "h": ("sbuf", [128, 4 * PICKS], "bfloat16"),
+    "hq": ("sbuf", [128, PICKS], CODES),
+    "hp": ("sbuf", [128, PICKS], BYTE),
+    "ys": ("sbuf", [128, PICKS], "float32"),
+    "ps": ("psum", [128, 4096], "float32"),
+}
+for _t in range(4):
+    SCRATCH["off%d" % _t] = ("sbuf", [128, 32], "uint16")
+    SCRATCH["res%d" % _t] = ("sbuf", [128, W + N * CAP], "bfloat16")
+SEMAPHORES = (["lst", "xin", "pkin", "win", "vin", "pad", "xqd", "vqd", "pkd", "loc"]
+              + [k + "%d" % i for k in ("wqd", "off", "gat", "sqd", "fill", "mo", "ro", "rs", "hg", "hq", "my", "cy", "out",
+                                        "arr", "ma", "mb", "mc", "ra", "rb", "rc") for i in range(4)])
+
+
+def mask_of(engines):
+    return sum(1 << e for e in engines)
+
+
+def groups_of(T, topo):
+    out = {}
+    for r, c in enumerate(T.cores):
+        out.setdefault(topo.chip(c), []).append(r)
+    return [out[k] for k in sorted(out, key=lambda k: out[k][0])]
+
+
+def ring(rank, step, T, topo):
+    groups = groups_of(T, topo)
+    mine = [i for i, q in enumerate(groups) if rank in q][0]
+    around = [(mine + step * k) % len(groups) for k in range(1, len(groups))]
+    near = [i for i in around if topo.same_plane(topo.chip(T.cores[rank]), topo.chip(T.cores[groups[i][0]]))]
+    return [i for i in around if i not in near] + near
+
+
+def place(dst, src, T, topo):
+    groups = groups_of(T, topo)
+    i = [n for n, q in enumerate(groups) if src in q][0]
+    if dst in groups[i]:
+        return W, i
+    return W + CAP + 2 * CAP * ring(dst, -1, T, topo).index(i) + CAP * groups[i].index(src), i
+
+
+def send(g, core, me, dests, at, T, topo):
+    far = [d for d in dests if topo.chip(T.cores[d]) != topo.chip(core)]
+    away = topo.engines(core, T.cores[far[0]])
+    share, total = len(away) // len(far), 0
+    for buf, land in (("sq", "cq"), ("sp", "cp")):
+        trs = []
+        for d in dests:
+            if d in far:
+                k = far.index(d)
+                eng = away[k * share:(k + 1) * share]
+            else:
+                eng = [e for e in topo.engines(core, T.cores[d]) if e not in away][:len(away)]
+            col, i = place(d, me, T, topo)
+            a, b = T[buf][:, at[d]:at[d] + CAP], T[land][:, col:col + CAP]
+            if buf == "sq":
+                a, b = a.bitcast(dt.uint8), b.bitcast(dt.uint8)
+            rid, pid, _ = topo.addr(T.cores[d])
+            trs.append(RemoteDMATransfer(dst_ids=[DstId(rid=rid, pnc=pid)], dma_engine_mask=mask_of(eng),
+                                         remote_sem=T.sem["arr%d" % i], src=a, dst=b))
+            total += len(eng)
+        g.remote_dma_fused(trs, local_sem=T.sem.loc)
+    return total
+
+
+def rank_program(g, core, T, topo):
+    rank = T.rank_of(core)
+    if rank is None:
+        return
+    S, V, A, E, Y = T.sem, g.vector, g.scalar, g.tensor, g.sync
+    COPY, RELU = ActivationFunctionType.Copy, ActivationFunctionType.Relu
+    groups = groups_of(T, topo)
+    mine = [i for i, q in enumerate(groups) if rank in q][0]
+    mate = [d for d in groups[mine] if d != rank][0]
+    steps = [list(groups[i]) for i in ring(rank, 1, T, topo)]
+    steps[1].append(mate)
+    at, pieces, col = {}, [], 0
+    for dests in steps:
+        runs, lo = [], col
+        for d in sorted(dests):
+            at[d] = col
+            if runs and runs[-1][1] == d:
+                runs[-1][1] = d + 1
+            else:
+                runs.append([d, d + 1, col])
+            col += CAP
+        pieces.append((runs, lo, col))
+
+    for q in range(8):
+        (Y if q < 4 else A).dma_start(T.lst[16 * q:16 * q + 16, :], T.snd[:, :]).then_inc(S.lst, 16)
+    Y.dma_start(T.xs[:, PAD:PAD + 4 * W], T.x[:, :]).then_inc(S.xin, 16)
+    Y.dma_start(T.ws[:], T.w[:, :]).then_inc(S.win, 16)
+    Y.dma_start(T.pkl[:], T.pk[:, :]).then_inc(S.pkin, 16)
+    Y.dma_start(T.vs[:], T.v[:, :]).then_inc(S.vin, 16)
+
+    V.memset(T.xs[:, 0:PAD], 0.0).then_inc(S.pad, 1)
+    V.wait_ge(S.lst, 128)
+    for t in (2, 0, 3, 1):
+        V.tensor_scalar(T["off%d" % t][:], T.lst[:], 4.0, float(PAD + t), AluOpType.mult, AluOpType.add).then_inc(S["off%d" % t], 1)
+    for b in range(4):
+        V.memset(T["res%d" % b][:, W + CAP * rank:W + CAP * rank + CAP], 0.0).then_inc(S["fill%d" % b], 1)
+
+    for q, ts in ((V, (0, 1)), (A, (2, 3, 1))):
+        q.wait_ge(S.pad, 1)
+        q.wait_ge(S.xin, 16)
+        for t in ts:
+            q.wait_ge(S["off%d" % t], 1)
+    sent = 0
+    for k, dests in enumerate(steps):
+        runs, lo, hi = pieces[k]
+        for t in range(4):
+            for d0, d1, c in runs:
+                out = T.gath[:, 4 * c + t:4 * (c + CAP * (d1 - d0)):4]
+                src = T.xs[:, 0:PAD + 4 * W].indirect(T["off%d" % t][:, 4 * d0:4 * d1])
+                if t < (2, 1, 2)[k]:
+                    V.tensor_copy(out, src).then_inc(S["gat%d" % k], 1)
+                else:
+                    A.activation(out, src, COPY).then_inc(S["gat%d" % k], 1)
+        V.wait_ge(S["gat%d" % k], 4 * len(runs))
+        V.quantize_mx(T.sq[:, lo:hi], T.sp[:, lo:hi], T.gath[:, 4 * lo:4 * hi]).then_inc(S["sqd%d" % k], 1)
+        if k == 0:
+            V.quantize_mx(T.cq[:, 0:W], T.cp[:, 0:W], T.xs[:, PAD:PAD + 4 * W]).then_inc(S.xqd, 1)
+        g.wait_ge(S["sqd%d" % k], 1)
+        sent += send(g, core, rank, dests, at, T, topo)
+    g.wait_ge(S.loc, sent)
+
+    V.wait_ge(S.win, 16)
+    for b in BS:
+        V.quantize_mx(T.wq[:, 128 * b:128 * b + 128], T.wp[:, 128 * b:128 * b + 128],
+                      T.ws[:, 512 * b:512 * b + 512]).then_inc(S["wqd%d" % b], 1)
+    V.wait_ge(S.vin, 16)
+    V.quantize_mx(T.vq[:], T.vp[:], T.vs[:]).then_inc(S.vqd, 1)
+    V.wait_ge(S.pkin, 16)
+    V.tensor_copy(T.pko[:], T.pkl[:]).then_inc(S.pkd, 1)
+
+    def product(b, bank, lo, hi, done):
+        E.matmul_mx(T.ps[:, 512 * bank:512 * bank + hi - lo], T.wq[:, 128 * b:128 * b + 128], T.wp[:, 128 * b:128 * b + 128],
+                    T.cq[:, lo:hi], T.cp[:, lo:hi], True, True).then_inc(S["%s%d" % (done, b)], 1)
+
+    def keep(b, bank, skip, lo, n, made, done):
+        q = V if b < 2 else A
+        q.wait_ge(S["%s%d" % (made, b)], 1)
+        src, out = T.ps[:, 512 * bank + skip:512 * bank + skip + n], T["res%d" % b][:, lo:lo + n]
+        if b < 2:
+            V.tensor_scalar(out, src, 0.0, 0.05, AluOpType.max, AluOpType.mult).then_inc(S["%s%d" % (done, b)], 1)
+        else:
+            A.activation(out, src, RELU, scale=0.05).then_inc(S["%s%d" % (done, b)], 1)
+
+    H, M = 320, 448
+
+    def ready(q, b):
+        for k in ("fill", "ro", "rs", "ra", "rb", "rc"):
+            q.wait_ge(S["%s%d" % (k, b)], 1)
+
+    def pick(q, b, lo, hi, done):
+        out = T.h[:, 4 * lo + b:4 * hi:4]
+        idx = T["res%d" % b][:, 0:W + N * CAP].indirect(T.pko[:, lo // 16:hi // 16])
+        if q is V:
+            V.tensor_copy(out, idx).then_inc(done, 1)
+        else:
+            A.activation(out, idx, COPY).then_inc(done, 1)
+
+    E.wait_ge(S.xqd, 1)
+    for b in BS:
+        E.wait_ge(S["wqd%d" % b], 1)
+        product(b, b, 0, W, "mo")
+        keep(b, b, 0, 0, W, "mo", "ro")
+    away = topo.engines(core, T.cores[groups[mine - 1][0]])
+    E.wait_ge(S["arr%d" % mine], 2 * len(away))
+    V.wait_ge(S.pkd, 1)
+    A.wait_ge(S.pkd, 1)
+    for n, i in enumerate(ring(rank, -1, T, topo)):
+        E.wait_ge(S["arr%d" % i], 2 * len(away))
+        lo, skip = W + CAP + 2 * CAP * n, 0 if n else CAP
+        made, done = ("ma", "mb", "mc")[n], ("ra", "rb", "rc")[n]
+        for b in BS:
+            bank = (4, 0, 4)[n] + b
+            for k in ((), ("ro",), ("rs", "ra"))[n]:
+                E.wait_ge(S["%s%d" % (k, b)], 1)
+            product(b, bank, lo - skip, lo + 2 * CAP, made)
+            if n == 0:
+                keep(b, bank, 0, W + CAP * mate, CAP, made, "rs")
+            keep(b, bank, skip, W + CAP * groups[i][0], 2 * CAP, made, done)
+            if n == 2:
+                q = V if b < 2 else A
+                ready(q, b)
+                pick(q, b, 0, H, S.hg0)
+
+    pick(V, 0, H, PICKS, S.hg1)
+    V.wait_ge(S.hg0, 4)
+    V.quantize_mx(T.hq[:, 0:H], T.hp[:, 0:H], T.h[:, 0:4 * H]).then_inc(S.hq0, 1)
+    pick(V, 1, H, M, S.hg1)
+    pick(A, 2, H, PICKS, S.hg1)
+    pick(A, 3, H, PICKS, S.hg1)
+    ready(A, 1)
+    pick(A, 1, M, PICKS, S.hg1)
+    V.wait_ge(S.hg1, 5)
+    V.quantize_mx(T.hq[:, H:PICKS], T.hp[:, H:PICKS], T.h[:, 4 * H:4 * PICKS]).then_inc(S.hq1, 1)
+    E.wait_ge(S.vqd, 1)
+    for n, (lo, hi) in enumerate(((0, H), (H, PICKS))):
+        E.wait_ge(S["hq%d" % n], 1)
+        E.wait_ge(S["rb%d" % n], 1)
+        src, out = T.ps[:, 512 * n:512 * n + hi - lo], T.ys[:, lo:hi]
+        E.matmul_mx(src, T.vq[:], T.vp[:], T.hq[:, lo:hi], T.hp[:, lo:hi], True, True).then_inc(S["my%d" % n], 1)
+        q = (A, V)[n]
+        q.wait_ge(S["my%d" % n], 1)
+        if q is A:
+            A.activation(out, src, COPY).then_inc(S["cy%d" % n], 1)
+        else:
+            V.tensor_copy(out, src).then_inc(S["cy%d" % n], 1)
+        Y.wait_ge(S["cy%d" % n], 1)
+        Y.dma_start(T.y[:, lo:hi], T.ys[:, lo:hi]).then_inc(S["out%d" % n], 16)
+    for n in range(2):
+        Y.wait_ge(S["out%d" % n], 16)

@@ -3,18 +3,24 @@ from concourse.mybir import dt, AluOpType, ActivationFunctionType
 
 N, W, CAP, PICKS = 8, 512, 64, 512
 PAD = 16
-BS = (0, 2, 1, 3)
 CODES, BYTE = "float8_e4m3fn_x4", "uint8"
+C = dict(
+    steps=(((0, 0), (0, 1)), ((1, 0), (1, 1), "M"), ((2, 0), (2, 1))),
+    road={((0, 1), "sq"): "near", ((0, 1), "sp"): "near"},
+    runs=(((0, 0), "M"), ((1, 0), (1, 1)), ((2, 0), (2, 1)), ((0, 1),)),
+    V="g00 g01 q0 g10 g11 q1 x04 g20 q2 w0 w2 w1 w3 k0 k1 p v", A="g02 g03 g12 g13 g21 g22 g23 k2 k3",
+    first=(1, 1, 1, 1), mcopy=True, wload=((0, 4),), parts=(0, 320, 512), M=448, vq_at=-1, heng=8, neng=8, feng=(8, 8, 8, 8), rbufs=("sq", "sp"),
+)
 SCRATCH = {
-    "lst": ("sbuf", [128, 32], "int32"),
+    "lst": ("sbuf", [128, 36], "int32"),
     "pkl": ("sbuf", [128, 32], "int32"),
     "pko": ("sbuf", [128, 32], "uint16"),
     "xs": ("sbuf", [128, PAD + 4 * W], "bfloat16"),
     "ws": ("sbuf", [128, 2048], "bfloat16"),
     "vs": ("sbuf", [128, 512], "bfloat16"),
-    "gath": ("sbuf", [128, 4 * 7 * CAP], "bfloat16"),
-    "sq": ("sbuf", [128, 7 * CAP], CODES),
-    "sp": ("sbuf", [128, 7 * CAP], BYTE),
+    "gath": ("sbuf", [128, 4 * 8 * CAP], "bfloat16"),
+    "sq": ("sbuf", [128, 8 * CAP], CODES),
+    "sp": ("sbuf", [128, 8 * CAP], BYTE),
     "cq": ("sbuf", [128, W + 7 * CAP], CODES),
     "cp": ("sbuf", [128, W + 7 * CAP], BYTE),
     "wq": ("sbuf", [128, 512], CODES),
@@ -28,11 +34,11 @@ SCRATCH = {
     "ps": ("psum", [128, 4096], "float32"),
 }
 for _t in range(4):
-    SCRATCH["off%d" % _t] = ("sbuf", [128, 32], "uint16")
+    SCRATCH["off%d" % _t] = ("sbuf", [128, 36], "uint16")
     SCRATCH["res%d" % _t] = ("sbuf", [128, W + N * CAP], "bfloat16")
-SEMAPHORES = (["lst", "xin", "pkin", "win", "vin", "pad", "xqd", "vqd", "pkd", "loc"]
-              + [k + "%d" % i for k in ("wqd", "off", "gat", "sqd", "fill", "mo", "ro", "rs", "hg", "hq", "my", "cy", "out",
-                                        "arr", "ma", "mb", "mc", "ra", "rb", "rc") for i in range(4)])
+SEMAPHORES = (["lst", "rep0", "rep1", "rep2", "xin", "pkin", "vin", "pad", "xqd", "vqd", "pkd", "loc"]
+              + [k + "%d" % i for k in ("sq", "sp", "win", "wqd", "off", "gat", "sqd", "fill", "mo", "ro", "hg", "hq", "my", "cy", "out",
+                                        "arr", "ma", "mb", "mc", "md", "ra", "rb", "rc", "rd") for i in range(4)])
 
 
 def mask_of(engines):
@@ -54,126 +60,269 @@ def ring(rank, step, T, topo):
     return [i for i in around if i not in near] + near
 
 
-def place(dst, src, T, topo):
-    groups = groups_of(T, topo)
-    i = [n for n, q in enumerate(groups) if src in q][0]
-    if dst in groups[i]:
-        return W, i
-    return W + CAP + 2 * CAP * ring(dst, -1, T, topo).index(i) + CAP * groups[i].index(src), i
+def peer(rank, unit, step, T, topo):
+    own = [q for q in groups_of(T, topo) if rank in q][0]
+    j = own.index(rank)
+    if unit == "M":
+        return own[1 - j]
+    return groups_of(T, topo)[ring(rank, step, T, topo)[unit[0]]][j ^ unit[1]]
 
 
-def send(g, core, me, dests, at, T, topo):
-    far = [d for d in dests if topo.chip(T.cores[d]) != topo.chip(core)]
-    away = topo.engines(core, T.cores[far[0]])
-    share, total = len(away) // len(far), 0
-    for buf, land in (("sq", "cq"), ("sp", "cp")):
-        trs = []
-        for d in dests:
-            if d in far:
-                k = far.index(d)
-                eng = away[k * share:(k + 1) * share]
-            else:
-                eng = [e for e in topo.engines(core, T.cores[d]) if e not in away][:len(away)]
-            col, i = place(d, me, T, topo)
-            a, b = T[buf][:, at[d]:at[d] + CAP], T[land][:, col:col + CAP]
-            if buf == "sq":
-                a, b = a.bitcast(dt.uint8), b.bitcast(dt.uint8)
-            rid, pid, _ = topo.addr(T.cores[d])
-            trs.append(RemoteDMATransfer(dst_ids=[DstId(rid=rid, pnc=pid)], dma_engine_mask=mask_of(eng),
-                                         remote_sem=T.sem["arr%d" % i], src=a, dst=b))
-            total += len(eng)
-        g.remote_dma_fused(trs, local_sem=T.sem.loc)
-    return total
+def layout(dst, T, topo):
+    out, col = {}, W
+    for n, run in enumerate(C["runs"]):
+        for u in sorted(run, key=lambda u: peer(dst, u, -1, T, topo)):
+            out[u] = (col, n)
+            col += CAP
+    return out
 
 
-def rank_program(g, core, T, topo):
-    rank = T.rank_of(core)
-    if rank is None:
-        return
-    S, V, A, E, Y = T.sem, g.vector, g.scalar, g.tensor, g.sync
-    COPY, RELU = ActivationFunctionType.Copy, ActivationFunctionType.Relu
-    groups = groups_of(T, topo)
-    mine = [i for i, q in enumerate(groups) if rank in q][0]
-    mate = [d for d in groups[mine] if d != rank][0]
-    steps = [list(groups[i]) for i in ring(rank, 1, T, topo)]
-    steps[1].append(mate)
+def helper(src, unit, buf, T, topo):
+    me, to = T.cores[src], T.cores[peer(src, unit, 1, T, topo)]
+    j = [q.index(src) for q in groups_of(T, topo) if src in q][0]
+    able = [c for c in topo.cores_of(me) if topo.die(c) != topo.die(me) and topo.may_write(c, to)]
+    return able[-2:][j] if C["road"][(unit, buf)] == "near" else able[j]
+
+
+def view(T, buf, lo, n):
+    a = T[buf][:, lo:lo + n]
+    return a.bitcast(dt.uint8) if buf in ("sq", "cq") else a
+
+
+def deal(core, targets, away, topo, cap=16):
+    far = [i for i, c in enumerate(targets) if topo.chip(c) != topo.chip(core)]
+    near = [i for i in range(len(targets)) if i not in far]
+    out = {}
+    for kind in (far, near):
+        for k, i in enumerate(kind):
+            eng = [e for e in topo.engines(core, targets[i]) if kind is far or e not in away][:cap if kind is far else C["neng"]]
+            share = 1
+            while 2 * share * len(kind) <= len(eng):
+                share *= 2
+            out[i] = eng[k * share:(k + 1) * share]
+    return [out[i] for i in range(len(targets))]
+
+
+def relayed(u, buf):
+    return (u, buf) in C["road"]
+
+
+def columns(rank, T, topo):
     at, pieces, col = {}, [], 0
-    for dests in steps:
+    mspot = peer(rank, "M", 1, T, topo)
+    for step in C["steps"]:
         runs, lo = [], col
-        for d in sorted(dests):
-            at[d] = col
+        spot = {u: peer(rank, u, 1, T, topo) for u in step}
+        if "M" in step and (1, 0) in step and C["mcopy"]:
+            spot["M"] = mspot = max(spot[(1, 0)], spot[(1, 1)]) + 1
+        for u in sorted(step, key=lambda u: spot[u]):
+            d = spot[u]
+            at[u] = col
             if runs and runs[-1][1] == d:
                 runs[-1][1] = d + 1
             else:
                 runs.append([d, d + 1, col])
             col += CAP
+        if col - lo < 2 * CAP:
+            col += CAP
         pieces.append((runs, lo, col))
+    return at, pieces, mspot
 
-    for q in range(8):
-        (Y if q < 4 else A).dma_start(T.lst[16 * q:16 * q + 16, :], T.snd[:, :]).then_inc(S.lst, 16)
+
+def plan(src, buf, T, topo):
+    core = T.cores[src]
+    away = topo.engines(core, T.cores[peer(src, (0, 0), 1, T, topo)])
+    at = columns(src, T, topo)[0]
+    out = []
+    for step in C["steps"]:
+        items = []
+        for u in sorted(step, key=lambda u: at[u]):
+            to = helper(src, u, buf, T, topo) if relayed(u, buf) else T.cores[peer(src, u, 1, T, topo)]
+            if items and items[-1][1] == to:
+                items[-1][0].append(u)
+            else:
+                items.append(([u], to))
+        calls = []
+        for n in sorted(set(len(i[0]) for i in items), reverse=True):
+            its = [i for i in items if len(i[0]) == n]
+            calls.append([(i[0], i[1], e) for i, e in zip(its, deal(core, [i[1] for i in its], away, topo, C["feng"][len(out)]))])
+        out.append(calls)
+    return out
+
+
+def handed(core, buf, k, T, topo):
+    jobs, adds = [], 0
+    for src in range(N):
+        if topo.chip(T.cores[src]) != topo.chip(core):
+            continue
+        for call in plan(src, buf, T, topo)[k]:
+            for units, to, eng in call:
+                if to == core and relayed(units[0], buf):
+                    adds += len(eng)
+                    jobs += [(src, u, T.cores[peer(src, u, 1, T, topo)]) for u in units]
+    if not jobs:
+        return [], 0
+    away = topo.engines(T.cores[jobs[0][0]], T.cores[peer(jobs[0][0], (0, 0), 1, T, topo)])
+    engs = deal(core, [j[2] for j in jobs], away, topo, C["heng"])
+    return [j + (e,) for j, e in zip(jobs, engs)], adds
+
+
+def transfer(T, topo, to, eng, sem, a, b):
+    rid, pid, _ = topo.addr(to)
+    return RemoteDMATransfer(dst_ids=[DstId(rid=rid, pnc=pid)], dma_engine_mask=mask_of(eng), remote_sem=sem, src=a, dst=b)
+
+
+def helper_program(g, core, T, topo):
+    total = 0
+    for k in range(len(C["steps"])):
+        for buf, land in (("sq", "cq"), ("sp", "cp"))[::C["first"][k]]:
+            jobs, adds = handed(core, buf, k, T, topo)
+            if not jobs:
+                continue
+            g.wait_ge(T.sem["%s%d" % (buf, k)], adds)
+            trs = []
+            for src, u, to, eng in jobs:
+                col, n = layout(T.rank_of(to), T, topo)[u]
+                a = view(T, buf, columns(src, T, topo)[0][u], CAP)
+                trs.append(transfer(T, topo, to, eng, T.sem["arr%d" % n], a, view(T, land, col, CAP)))
+                total += len(eng)
+            g.remote_dma_fused(trs, local_sem=T.sem.loc)
+    if total:
+        g.wait_ge(T.sem.loc, total)
+
+
+def expected(rank, T, topo):
+    out = [0] * len(C["runs"])
+    for u, (col, n) in layout(rank, T, topo).items():
+        src = peer(rank, u, -1, T, topo)
+        for buf in ("sq", "sp"):
+            if relayed(u, buf):
+                k = [u in step for step in C["steps"]].index(True)
+                out[n] += [len(j[3]) for j in handed(helper(src, u, buf, T, topo), buf, k, T, topo)[0] if j[:2] == (src, u)][0]
+            else:
+                out[n] += [len(e) for calls in plan(src, buf, T, topo) for call in calls for us, to, e in call if us == [u]][0]
+    return out
+
+
+def rank_program(g, core, T, topo):
+    rank = T.rank_of(core)
+    if rank is None:
+        return helper_program(g, core, T, topo)
+    S, V, A, E, Y = T.sem, g.vector, g.scalar, g.tensor, g.sync
+    COPY, RELU = ActivationFunctionType.Copy, ActivationFunctionType.Relu
+    BS = (0, 2, 1, 3)
+    mate = peer(rank, "M", 1, T, topo)
+    at, pieces, mspot = columns(rank, T, topo)
+
+    for q in range(2):
+        (Y, A)[q].dma_start(T.lst[16 * q:16 * q + 16, 0:32], T.snd[:, :]).then_inc(S.lst, 16)
     Y.dma_start(T.xs[:, PAD:PAD + 4 * W], T.x[:, :]).then_inc(S.xin, 16)
-    Y.dma_start(T.ws[:], T.w[:, :]).then_inc(S.win, 16)
+    wsem = {}
+    for j, (b0, b1) in enumerate(C["wload"]):
+        Y.dma_start(T.ws[:, 512 * b0:512 * b1], T.w[:, 512 * b0:512 * b1]).then_inc(S["win%d" % j], 16)
+        for b in range(b0, b1):
+            wsem[b] = S["win%d" % j]
     Y.dma_start(T.pkl[:], T.pk[:, :]).then_inc(S.pkin, 16)
     Y.dma_start(T.vs[:], T.v[:, :]).then_inc(S.vin, 16)
 
     V.memset(T.xs[:, 0:PAD], 0.0).then_inc(S.pad, 1)
-    V.wait_ge(S.lst, 128)
-    for t in (2, 0, 3, 1):
-        V.tensor_scalar(T["off%d" % t][:], T.lst[:], 4.0, float(PAD + t), AluOpType.mult, AluOpType.add).then_inc(S["off%d" % t], 1)
+    pads = 1
+    for k, step in enumerate(C["steps"]):
+        if len(step) < 2:
+            V.memset(T.gath[:, 4 * (pieces[k][2] - CAP):4 * pieces[k][2]], 0.0).then_inc(S.pad, 1)
+            pads += 1
     for b in range(4):
         V.memset(T["res%d" % b][:, W + CAP * rank:W + CAP * rank + CAP], 0.0).then_inc(S["fill%d" % b], 1)
+    V.wait_ge(S.lst, 32)
+    wid = max(32, 4 * mspot + 4)
+    if mspot != mate:
+        V.tensor_copy(T.lst[0:32, 4 * mspot:4 * mspot + 4], T.lst[0:32, 4 * mate:4 * mate + 4]).then_inc(S.rep2, 1)
+        V.wait_ge(S.rep2, 1)
+    for q in range(1, 4):
+        V.tensor_copy(T.lst[32 * q:32 * q + 32, 0:wid], T.lst[0:32, 0:wid]).then_inc(S.rep0, 1)
+    V.wait_ge(S.rep0, 3)
+    for t in (2, 0, 3, 1):
+        V.tensor_scalar(T["off%d" % t][:, 0:wid], T.lst[:, 0:wid], 4.0, float(PAD + t), AluOpType.mult,
+                        AluOpType.add).then_inc(S["off%d" % t], 1)
 
-    for q, ts in ((V, (0, 1)), (A, (2, 3, 1))):
-        q.wait_ge(S.pad, 1)
+    for q in (V, A):
+        q.wait_ge(S.pad, pads)
         q.wait_ge(S.xin, 16)
-        for t in ts:
-            q.wait_ge(S["off%d" % t], 1)
-    sent = 0
-    for k, dests in enumerate(steps):
-        runs, lo, hi = pieces[k]
         for t in range(4):
-            for d0, d1, c in runs:
-                out = T.gath[:, 4 * c + t:4 * (c + CAP * (d1 - d0)):4]
-                src = T.xs[:, 0:PAD + 4 * W].indirect(T["off%d" % t][:, 4 * d0:4 * d1])
-                if t < (2, 1, 2)[k]:
-                    V.tensor_copy(out, src).then_inc(S["gat%d" % k], 1)
-                else:
-                    A.activation(out, src, COPY).then_inc(S["gat%d" % k], 1)
-        V.wait_ge(S["gat%d" % k], 4 * len(runs))
-        V.quantize_mx(T.sq[:, lo:hi], T.sp[:, lo:hi], T.gath[:, 4 * lo:4 * hi]).then_inc(S["sqd%d" % k], 1)
-        if k == 0:
-            V.quantize_mx(T.cq[:, 0:W], T.cp[:, 0:W], T.xs[:, PAD:PAD + 4 * W]).then_inc(S.xqd, 1)
-        g.wait_ge(S["sqd%d" % k], 1)
-        sent += send(g, core, rank, dests, at, T, topo)
-    g.wait_ge(S.loc, sent)
+            q.wait_ge(S["off%d" % t], 1)
 
-    V.wait_ge(S.win, 16)
-    for b in BS:
+    def quant_w(b):
+        V.wait_ge(wsem[b], 16)
         V.quantize_mx(T.wq[:, 128 * b:128 * b + 128], T.wp[:, 128 * b:128 * b + 128],
                       T.ws[:, 512 * b:512 * b + 512]).then_inc(S["wqd%d" % b], 1)
-    V.wait_ge(S.vin, 16)
-    V.quantize_mx(T.vq[:], T.vp[:], T.vs[:]).then_inc(S.vqd, 1)
-    V.wait_ge(S.pkin, 16)
-    V.tensor_copy(T.pko[:], T.pkl[:]).then_inc(S.pkd, 1)
+
+    def gather(q, k, t):
+        for d0, d1, c in pieces[k][0]:
+            out = T.gath[:, 4 * c + t:4 * (c + CAP * (d1 - d0)):4]
+            src = T.xs[:, 0:PAD + 4 * W].indirect(T["off%d" % t][:, 4 * d0:4 * d1])
+            if q is V:
+                V.tensor_copy(out, src).then_inc(S["gat%d" % k], 1)
+            else:
+                A.activation(out, src, COPY).then_inc(S["gat%d" % k], 1)
+
+    def keep(q, b, bank, skip, lo, n, done):
+        src, out = T.ps[:, 512 * bank + skip:512 * bank + skip + n], T["res%d" % b][:, lo:lo + n]
+        if q is V:
+            V.tensor_scalar(out, src, 0.0, 0.05, AluOpType.max, AluOpType.mult).then_inc(S["%s%d" % (done, b)], 1)
+        else:
+            A.activation(out, src, RELU, scale=0.05).then_inc(S["%s%d" % (done, b)], 1)
+
+    for q, words in ((V, C["V"]), (A, C["A"])):
+        for word in words.split():
+            op, n = word[0], [int(c) for c in word[1:]]
+            if op == "g":
+                gather(q, n[0], n[1])
+            elif op == "q":
+                runs, lo, hi = pieces[n[0]]
+                V.wait_ge(S["gat%d" % n[0]], 4 * len(runs))
+                V.quantize_mx(T.sq[:, lo:hi], T.sp[:, lo:hi], T.gath[:, 4 * lo:4 * hi]).then_inc(S["sqd%d" % n[0]], 1)
+            elif op == "x":
+                lo, hi = 128 * n[0], 128 * n[1]
+                V.quantize_mx(T.cq[:, lo:hi], T.cp[:, lo:hi], T.xs[:, PAD + 4 * lo:PAD + 4 * hi]).then_inc(S.xqd, n[1] - n[0])
+            elif op == "w":
+                quant_w(n[0])
+            elif op == "k":
+                q.wait_ge(S["mo%d" % n[0]], 1)
+                keep(q, n[0], n[0], 0, 0, W, "ro")
+            elif op == "p":
+                V.wait_ge(S.pkin, 16)
+                V.tensor_copy(T.pko[:], T.pkl[:]).then_inc(S.pkd, 1)
+            elif op == "v":
+                V.wait_ge(S.vin, 16)
+                V.quantize_mx(T.vq[:], T.vp[:], T.vs[:]).then_inc(S.vqd, 1)
+
+    sent = 0
+    for k in range(len(C["steps"])):
+        g.wait_ge(S["sqd%d" % k], 1)
+        for buf, land in (("sq", "cq"), ("sp", "cp"))[::C["first"][k]]:
+            for call in plan(rank, buf, T, topo)[k]:
+                trs = []
+                for units, to, eng in call:
+                    a = view(T, buf, at[units[0]], CAP * len(units))
+                    if relayed(units[0], buf):
+                        trs.append(transfer(T, topo, to, eng, S["%s%d" % (buf, k)], a, a))
+                    else:
+                        colm, n = layout(T.rank_of(to), T, topo)[units[0]]
+                        trs.append(transfer(T, topo, to, eng, S["arr%d" % n], a, view(T, land, colm, CAP)))
+                    sent += len(eng)
+                g.remote_dma_fused(trs, local_sem=S.loc)
+    g.wait_ge(S.loc, sent)
 
     def product(b, bank, lo, hi, done):
         E.matmul_mx(T.ps[:, 512 * bank:512 * bank + hi - lo], T.wq[:, 128 * b:128 * b + 128], T.wp[:, 128 * b:128 * b + 128],
                     T.cq[:, lo:hi], T.cp[:, lo:hi], True, True).then_inc(S["%s%d" % (done, b)], 1)
 
-    def keep(b, bank, skip, lo, n, made, done):
-        q = V if b < 2 else A
-        q.wait_ge(S["%s%d" % (made, b)], 1)
-        src, out = T.ps[:, 512 * bank + skip:512 * bank + skip + n], T["res%d" % b][:, lo:lo + n]
-        if b < 2:
-            V.tensor_scalar(out, src, 0.0, 0.05, AluOpType.max, AluOpType.mult).then_inc(S["%s%d" % (done, b)], 1)
-        else:
-            A.activation(out, src, RELU, scale=0.05).then_inc(S["%s%d" % (done, b)], 1)
-
-    H, M = 320, 448
+    lay = layout(rank, T, topo)
+    kept = {"fill": 1, "ro": 1}
 
     def ready(q, b):
-        for k in ("fill", "ro", "rs", "ra", "rb", "rc"):
-            q.wait_ge(S["%s%d" % (k, b)], 1)
+        for k in kept:
+            q.wait_ge(S["%s%d" % (k, b)], kept[k])
 
     def pick(q, b, lo, hi, done):
         out = T.h[:, 4 * lo + b:4 * hi:4]
@@ -183,49 +332,58 @@ def rank_program(g, core, T, topo):
         else:
             A.activation(out, idx, COPY).then_inc(done, 1)
 
-    E.wait_ge(S.xqd, 1)
-    for b in BS:
+    E.wait_ge(S.xqd, 4)
+    for b in [int(word[1]) for word in C["V"].split() if word[0] == "w"]:
         E.wait_ge(S["wqd%d" % b], 1)
         product(b, b, 0, W, "mo")
-        keep(b, b, 0, 0, W, "mo", "ro")
-    away = topo.engines(core, T.cores[groups[mine - 1][0]])
-    E.wait_ge(S["arr%d" % mine], 2 * len(away))
-    V.wait_ge(S.pkd, 1)
-    A.wait_ge(S.pkd, 1)
-    for n, i in enumerate(ring(rank, -1, T, topo)):
-        E.wait_ge(S["arr%d" % i], 2 * len(away))
-        lo, skip = W + CAP + 2 * CAP * n, 0 if n else CAP
-        made, done = ("ma", "mb", "mc")[n], ("ra", "rb", "rc")[n]
-        for b in BS:
-            bank = (4, 0, 4)[n] + b
-            for k in ((), ("ro",), ("rs", "ra"))[n]:
-                E.wait_ge(S["%s%d" % (k, b)], 1)
-            product(b, bank, lo - skip, lo + 2 * CAP, made)
-            if n == 0:
-                keep(b, bank, 0, W + CAP * mate, CAP, made, "rs")
-            keep(b, bank, skip, W + CAP * groups[i][0], 2 * CAP, made, done)
-            if n == 2:
-                q = V if b < 2 else A
-                ready(q, b)
-                pick(q, b, 0, H, S.hg0)
 
-    pick(V, 0, H, PICKS, S.hg1)
-    V.wait_ge(S.hg0, 4)
-    V.quantize_mx(T.hq[:, 0:H], T.hp[:, 0:H], T.h[:, 0:4 * H]).then_inc(S.hq0, 1)
-    pick(V, 1, H, M, S.hg1)
-    pick(A, 2, H, PICKS, S.hg1)
-    pick(A, 3, H, PICKS, S.hg1)
-    ready(A, 1)
-    pick(A, 1, M, PICKS, S.hg1)
-    V.wait_ge(S.hg1, 5)
-    V.quantize_mx(T.hq[:, H:PICKS], T.hp[:, H:PICKS], T.h[:, 4 * H:4 * PICKS]).then_inc(S.hq1, 1)
+    parts = C["parts"]
+    nr = len(C["runs"])
+    exp = expected(rank, T, topo)
+    last_user = {0: "ro"}
+    for n, run in enumerate(C["runs"]):
+        if n == C["vq_at"]:
+            V.wait_ge(S.vin, 16)
+            V.quantize_mx(T.vq[:], T.vp[:], T.vs[:]).then_inc(S.vqd, 1)
+        E.wait_ge(S["arr%d" % n], exp[n])
+        lo = min(lay[u][0] for u in run)
+        hi = lo + CAP * len(run)
+        back = CAP if len(run) < 2 else 0
+        segs = []
+        for u in sorted(run, key=lambda u: lay[u][0]):
+            s = peer(rank, u, -1, T, topo)
+            if segs and segs[-1][1] + segs[-1][2] == W + CAP * s:
+                segs[-1][2] += CAP
+            else:
+                segs.append([lay[u][0] - lo + back, W + CAP * s, CAP])
+        made, done = "m" + "abcd"[n], "r" + "abcd"[n]
+        kept[done] = len(segs)
+        half = 4 * ((n + 1) % 2)
+        for b in BS:
+            q = V if b in C.get("fkeep", ((0, 1),) * 4)[n] else A
+            if half in last_user:
+                E.wait_ge(S["%s%d" % (last_user[half], b)], kept[last_user[half]])
+            product(b, half + b, lo - back, hi, made)
+            q.wait_ge(S["%s%d" % (made, b)], 1)
+            for skip, to, cnt in segs:
+                keep(q, b, half + b, skip, to, cnt, done)
+        for b in BS:
+            if n == nr - 1:
+                q = V if b < 2 else A
+                if b in (0, 2):
+                    q.wait_ge(S.pkd, 1)
+                ready(q, b)
+                pick(q, b, 0, parts[1], S.hg0)
+        last_user[half] = done
+
+    np_ = len(parts) - 1
     E.wait_ge(S.vqd, 1)
-    for n, (lo, hi) in enumerate(((0, H), (H, PICKS))):
-        E.wait_ge(S["hq%d" % n], 1)
-        E.wait_ge(S["rb%d" % n], 1)
-        src, out = T.ps[:, 512 * n:512 * n + hi - lo], T.ys[:, lo:hi]
-        E.matmul_mx(src, T.vq[:], T.vp[:], T.hq[:, lo:hi], T.hp[:, lo:hi], True, True).then_inc(S["my%d" % n], 1)
-        q = (A, V)[n]
+    aready = [False]
+    free = 4 * (nr % 2 == 0)
+
+    def copy_out(n, q):
+        lo, hi = parts[n], parts[n + 1]
+        src, out = T.ps[:, 512 * (free + n):512 * (free + n) + hi - lo], T.ys[:, lo:hi]
         q.wait_ge(S["my%d" % n], 1)
         if q is A:
             A.activation(out, src, COPY).then_inc(S["cy%d" % n], 1)
@@ -233,5 +391,37 @@ def rank_program(g, core, T, topo):
             V.tensor_copy(out, src).then_inc(S["cy%d" % n], 1)
         Y.wait_ge(S["cy%d" % n], 1)
         Y.dma_start(T.y[:, lo:hi], T.ys[:, lo:hi]).then_inc(S["out%d" % n], 16)
-    for n in range(2):
+
+    def quant_h(n, cnt):
+        lo, hi = parts[n], parts[n + 1]
+        V.wait_ge(S["hg%d" % n], cnt)
+        V.quantize_mx(T.hq[:, lo:hi], T.hp[:, lo:hi], T.h[:, 4 * lo:4 * hi]).then_inc(S["hq%d" % n], 1)
+        E.wait_ge(S["hq%d" % n], 1)
+        E.wait_ge(S["%s%d" % (last_user[free], n)], kept[last_user[free]])
+        E.matmul_mx(T.ps[:, 512 * (free + n):512 * (free + n) + hi - lo], T.vq[:], T.vp[:], T.hq[:, lo:hi], T.hp[:, lo:hi],
+                    True, True).then_inc(S["my%d" % n], 1)
+
+    cnt = 4
+    Ms = C["M"] if isinstance(C["M"], tuple) else (C["M"],)
+    for n in range(1, np_):
+        lo, hi, M = parts[n], parts[n + 1], Ms[n - 1]
+        s = S["hg%d" % n]
+        pick(V, 0, lo, hi, s)
+        quant_h(n - 1, cnt)
+        cnt = 3
+        if M > lo:
+            pick(V, 1, lo, M, s)
+            cnt += 1
+        pick(A, 2, lo, hi, s)
+        pick(A, 3, lo, hi, s)
+        if M < hi:
+            if not aready[0]:
+                ready(A, 1)
+                aready[0] = True
+            pick(A, 1, M, hi, s)
+            cnt += 1
+        copy_out(n - 1, A)
+    quant_h(np_ - 1, cnt)
+    copy_out(np_ - 1, V)
+    for n in range(np_):
         Y.wait_ge(S["out%d" % n], 16)

@@ -3,24 +3,29 @@ from concourse.mybir import dt, AluOpType, ActivationFunctionType
 
 N, W, CAP, PICKS = 8, 512, 64, 512
 PAD = 16
+PART = 128
 CODES, BYTE = "float8_e4m3fn_x4", "uint8"
 C = dict(
-    steps=(((0, 0), (0, 1)), ((1, 0), (1, 1), "M"), ((2, 0), (2, 1))),
-    road={((0, 1), "sq"): "near", ((0, 1), "sp"): "near"},
-    runs=(((0, 0), "M"), ((1, 0), (1, 1)), ((2, 0), (2, 1)), ((0, 1),)),
-    V="g00 g01 q0 g10 g11 q1 x04 g20 q2 w0 w2 w1 w3 k0 k1 p v", A="g02 g03 g12 g13 g21 g22 g23 k2 k3",
-    first=(1, 1, 1, 1), mcopy=True, wload=((0, 4),), parts=(0, 320, 512), M=448, vq_at=-1, heng=8, neng=8, feng=(8, 8, 8, 8), rbufs=("sq", "sp"),
+    steps=(("a", "c0"), ("b0", "b1", "m"), ("e", "c1")),
+    calls=("q a c0", "p a c0", "q b0 b1 m", "p e c1", "p b0 b1 m", "q e", "q c1"),
+    road={"q c0": 0, "p c0": 1, "p c1": 0}, halves={0: (0, 4, 1), 1: (4, 8, 1)}, neng=8,
+    runs=(("a", "m"), ("b0", "b1"), ("e",), ("c0", "c1")),
+    V="g00 g01 q0 g10 g11 x01 q1 x14 w2 q2 w3 w0 w1 p v k0", A="g02 g03 g12 g13 g20 g21 g22 g23 k2 k3 k1",
+    fkeep=((0, 1, 2), (0, 1), (0, 1), (0, 1)),
+    TV=(("p", 0, 0, 256), ("p", 1, 0, 416), ("p", 3, 192, 384), ("q", 0), ("q", 1), ("p", 1, 416, 512), ("q", 2), ("q", 3),
+        ("c", 3)),
+    TA=(("p", 2, 0, 512), ("p", 3, 0, 192), ("p", 0, 256, 512), ("p", 3, 384, 512), ("c", 0), ("c", 1), ("c", 2)),
 )
 SCRATCH = {
-    "lst": ("sbuf", [128, 36], "int32"),
+    "lst": ("sbuf", [128, 4 * (N + 2)], "int32"),
     "pkl": ("sbuf", [128, 32], "int32"),
     "pko": ("sbuf", [128, 32], "uint16"),
     "xs": ("sbuf", [128, PAD + 4 * W], "bfloat16"),
     "ws": ("sbuf", [128, 2048], "bfloat16"),
     "vs": ("sbuf", [128, 512], "bfloat16"),
-    "gath": ("sbuf", [128, 4 * 8 * CAP], "bfloat16"),
-    "sq": ("sbuf", [128, 8 * CAP], CODES),
-    "sp": ("sbuf", [128, 8 * CAP], BYTE),
+    "gath": ("sbuf", [128, 4 * 7 * CAP], "bfloat16"),
+    "sq": ("sbuf", [128, 7 * CAP], CODES),
+    "sp": ("sbuf", [128, 7 * CAP], BYTE),
     "cq": ("sbuf", [128, W + 7 * CAP], CODES),
     "cp": ("sbuf", [128, W + 7 * CAP], BYTE),
     "wq": ("sbuf", [128, 512], CODES),
@@ -34,15 +39,12 @@ SCRATCH = {
     "ps": ("psum", [128, 4096], "float32"),
 }
 for _t in range(4):
-    SCRATCH["off%d" % _t] = ("sbuf", [128, 36], "uint16")
+    SCRATCH["off%d" % _t] = ("sbuf", [128, 4 * (N + 2)], "uint16")
     SCRATCH["res%d" % _t] = ("sbuf", [128, W + N * CAP], "bfloat16")
-SEMAPHORES = (["lst", "rep0", "rep1", "rep2", "xin", "pkin", "vin", "pad", "xqd", "vqd", "pkd", "loc"]
-              + [k + "%d" % i for k in ("sq", "sp", "win", "wqd", "off", "gat", "sqd", "fill", "mo", "ro", "hg", "hq", "my", "cy", "out",
+SEMAPHORES = (["lst", "moved", "spread", "xin", "win", "pkin", "vin", "pad", "xqd", "vqd", "pkd", "loc"]
+              + [k + "%d" % i for k in ("hg", "hand") for i in range(10)]
+              + [k + "%d" % i for k in ("wqd", "off", "gat", "sqd", "fill", "mo", "ro", "hq", "my", "cy", "out",
                                         "arr", "ma", "mb", "mc", "md", "ra", "rb", "rc", "rd") for i in range(4)])
-
-
-def mask_of(engines):
-    return sum(1 << e for e in engines)
 
 
 def groups_of(T, topo):
@@ -52,155 +54,119 @@ def groups_of(T, topo):
     return [out[k] for k in sorted(out, key=lambda k: out[k][0])]
 
 
-def ring(rank, step, T, topo):
+def peer(rank, name, T, topo):
     groups = groups_of(T, topo)
-    mine = [i for i, q in enumerate(groups) if rank in q][0]
-    around = [(mine + step * k) % len(groups) for k in range(1, len(groups))]
-    near = [i for i in around if topo.same_plane(topo.chip(T.cores[rank]), topo.chip(T.cores[groups[i][0]]))]
-    return [i for i in around if i not in near] + near
+    m = [rank in q for q in groups].index(True)
+    j = groups[m].index(rank)
+    way = 2 * j - 1
+    if name == "m":
+        return groups[m][1 - j]
+    if name[0] == "c":
+        plane = [q for q in groups if topo.same_plane(topo.chip(T.cores[q[0]]), topo.chip(T.cores[rank]))][0]
+        return plane[j ^ int(name[1])]
+    if name[0] == "b":
+        return groups[(m - way) % len(groups)][int(name[1])]
+    return groups[(m + way) % len(groups)][1 - j if name == "a" else j]
 
 
-def peer(rank, unit, step, T, topo):
-    own = [q for q in groups_of(T, topo) if rank in q][0]
-    j = own.index(rank)
-    if unit == "M":
-        return own[1 - j]
-    return groups_of(T, topo)[ring(rank, step, T, topo)[unit[0]]][j ^ unit[1]]
+def gathered(rank, T, topo):
+    at, steps, moves, col = {}, [], [], 0
+    for step in C["steps"]:
+        place = {u: 1 + peer(rank, u, T, topo) for u in step}
+        beside = [min(place[u] for u in step[:-1]) - 1, max(place[u] for u in step[:-1]) + 1]
+        if place[step[-1]] not in beside:
+            free = [i for i in beside if i in (0, 1 + rank, N + 1)][0]
+            moves.append((free, place[step[-1]]))
+            place[step[-1]] = free
+        low = min(place.values())
+        for u in step:
+            at[u] = col + CAP * (place[u] - low)
+        steps.append((low, low + len(step), col, col + CAP * len(step)))
+        col += CAP * len(step)
+    return at, steps, moves
 
 
-def layout(dst, T, topo):
+def landing(dst, T, topo):
     out, col = {}, W
     for n, run in enumerate(C["runs"]):
-        for u in sorted(run, key=lambda u: peer(dst, u, -1, T, topo)):
-            out[u] = (col, n)
-            col += CAP
+        for s in range(N):
+            if dst in [peer(s, u, T, topo) for u in run]:
+                out[s] = (col, n)
+                col += CAP
     return out
 
 
-def helper(src, unit, buf, T, topo):
-    me, to = T.cores[src], T.cores[peer(src, unit, 1, T, topo)]
+def helper(src, which, T, topo):
+    me = T.cores[src]
     j = [q.index(src) for q in groups_of(T, topo) if src in q][0]
-    able = [c for c in topo.cores_of(me) if topo.die(c) != topo.die(me) and topo.may_write(c, to)]
-    return able[-2:][j] if C["road"][(unit, buf)] == "near" else able[j]
+    return [c for c in topo.cores_of(me) if topo.die(c) != topo.die(me)][2 * which + j]
 
 
-def view(T, buf, lo, n):
-    a = T[buf][:, lo:lo + n]
-    return a.bitcast(dt.uint8) if buf in ("sq", "cq") else a
-
-
-def deal(core, targets, away, topo, cap=16):
-    far = [i for i, c in enumerate(targets) if topo.chip(c) != topo.chip(core)]
-    near = [i for i in range(len(targets)) if i not in far]
-    out = {}
-    for kind in (far, near):
-        for k, i in enumerate(kind):
-            eng = [e for e in topo.engines(core, targets[i]) if kind is far or e not in away][:cap if kind is far else C["neng"]]
-            share = 1
-            while 2 * share * len(kind) <= len(eng):
-                share *= 2
-            out[i] = eng[k * share:(k + 1) * share]
-    return [out[i] for i in range(len(targets))]
-
-
-def relayed(u, buf):
-    return (u, buf) in C["road"]
-
-
-def columns(rank, T, topo):
-    at, pieces, col = {}, [], 0
-    mspot = peer(rank, "M", 1, T, topo)
-    for step in C["steps"]:
-        runs, lo = [], col
-        spot = {u: peer(rank, u, 1, T, topo) for u in step}
-        if "M" in step and (1, 0) in step and C["mcopy"]:
-            spot["M"] = mspot = max(spot[(1, 0)], spot[(1, 1)]) + 1
-        for u in sorted(step, key=lambda u: spot[u]):
-            d = spot[u]
-            at[u] = col
-            if runs and runs[-1][1] == d:
-                runs[-1][1] = d + 1
-            else:
-                runs.append([d, d + 1, col])
-            col += CAP
-        if col - lo < 2 * CAP:
-            col += CAP
-        pieces.append((runs, lo, col))
-    return at, pieces, mspot
-
-
-def plan(src, buf, T, topo):
-    core = T.cores[src]
-    away = topo.engines(core, T.cores[peer(src, (0, 0), 1, T, topo)])
-    at = columns(src, T, topo)[0]
-    out = []
-    for step in C["steps"]:
+def writes(src, T, topo):
+    core, out = T.cores[src], []
+    away = topo.engines(core, T.cores[peer(src, "a", T, topo)])
+    for call in C["calls"]:
+        kind, names = call.split()[0], call.split()[1:]
+        road = {u: C["road"].get(kind + " " + u) for u in names}
+        to = {u: T.cores[peer(src, u, T, topo)] if road[u] is None else helper(src, road[u], T, topo) for u in names}
+        far = [u for u in names if topo.chip(to[u]) != topo.chip(core)]
         items = []
-        for u in sorted(step, key=lambda u: at[u]):
-            to = helper(src, u, buf, T, topo) if relayed(u, buf) else T.cores[peer(src, u, 1, T, topo)]
-            if items and items[-1][1] == to:
-                items[-1][0].append(u)
-            else:
-                items.append(([u], to))
-        calls = []
-        for n in sorted(set(len(i[0]) for i in items), reverse=True):
-            its = [i for i in items if len(i[0]) == n]
-            calls.append([(i[0], i[1], e) for i, e in zip(its, deal(core, [i[1] for i in its], away, topo, C["feng"][len(out)]))])
-        out.append(calls)
+        for u in names:
+            like = far if u in far else [v for v in names if v not in far]
+            eng = away if u in far else [e for e in topo.engines(core, to[u]) if e not in away][::8 // C["neng"]]
+            if u in far and len(out) in C["halves"]:
+                eng = eng[C["halves"][len(out)][0]:C["halves"][len(out)][1]:C["halves"][len(out)][2]]
+            share = 1
+            while 2 * share * len(like) <= len(eng):
+                share *= 2
+            k = like.index(u)
+            items.append((u, to[u], eng[k * share:(k + 1) * share], road[u] is not None))
+        out.append((kind, items))
     return out
 
 
-def handed(core, buf, k, T, topo):
-    jobs, adds = [], 0
-    for src in range(N):
-        if topo.chip(T.cores[src]) != topo.chip(core):
-            continue
-        for call in plan(src, buf, T, topo)[k]:
-            for units, to, eng in call:
-                if to == core and relayed(units[0], buf):
-                    adds += len(eng)
-                    jobs += [(src, u, T.cores[peer(src, u, 1, T, topo)]) for u in units]
-    if not jobs:
-        return [], 0
-    away = topo.engines(T.cores[jobs[0][0]], T.cores[peer(jobs[0][0], (0, 0), 1, T, topo)])
-    engs = deal(core, [j[2] for j in jobs], away, topo, C["heng"])
-    return [j + (e,) for j, e in zip(jobs, engs)], adds
+def view(T, kind, landed, lo):
+    if kind == "q":
+        return T["cq" if landed else "sq"][:, lo:lo + CAP].bitcast(dt.uint8)
+    return T["cp" if landed else "sp"][:, lo:lo + CAP]
 
 
-def transfer(T, topo, to, eng, sem, a, b):
+def transfer(topo, to, engines, sem, a, b):
     rid, pid, _ = topo.addr(to)
-    return RemoteDMATransfer(dst_ids=[DstId(rid=rid, pnc=pid)], dma_engine_mask=mask_of(eng), remote_sem=sem, src=a, dst=b)
+    return RemoteDMATransfer(dst_ids=[DstId(rid=rid, pnc=pid)], dma_engine_mask=sum(1 << e for e in engines),
+                             remote_sem=sem, src=a, dst=b)
+
+
+def onward(core, job, to, topo):
+    jobs = [j for j in C["road"] if C["road"][j] == C["road"][job]]
+    return topo.engines(core, to)[jobs.index(job)::2]
 
 
 def helper_program(g, core, T, topo):
     total = 0
-    for k in range(len(C["steps"])):
-        for buf, land in (("sq", "cq"), ("sp", "cp"))[::C["first"][k]]:
-            jobs, adds = handed(core, buf, k, T, topo)
-            if not jobs:
-                continue
-            g.wait_ge(T.sem["%s%d" % (buf, k)], adds)
-            trs = []
-            for src, u, to, eng in jobs:
-                col, n = layout(T.rank_of(to), T, topo)[u]
-                a = view(T, buf, columns(src, T, topo)[0][u], CAP)
-                trs.append(transfer(T, topo, to, eng, T.sem["arr%d" % n], a, view(T, land, col, CAP)))
-                total += len(eng)
-            g.remote_dma_fused(trs, local_sem=T.sem.loc)
+    for src in range(N):
+        for i, (kind, items) in enumerate(writes(src, T, topo)):
+            for u, to, eng, handed in items:
+                if handed and to == core:
+                    dst = peer(src, u, T, topo)
+                    col, n = landing(dst, T, topo)[src]
+                    away = onward(core, kind + " " + u, T.cores[dst], topo)
+                    g.wait_ge(T.sem["hand%d" % i], len(eng))
+                    g.remote_dma_fused([transfer(topo, T.cores[dst], away, T.sem["arr%d" % n],
+                                                 view(T, kind, False, gathered(src, T, topo)[0][u]), view(T, kind, True, col))],
+                                       local_sem=T.sem.loc)
+                    total += len(away)
     if total:
         g.wait_ge(T.sem.loc, total)
 
 
 def expected(rank, T, topo):
     out = [0] * len(C["runs"])
-    for u, (col, n) in layout(rank, T, topo).items():
-        src = peer(rank, u, -1, T, topo)
-        for buf in ("sq", "sp"):
-            if relayed(u, buf):
-                k = [u in step for step in C["steps"]].index(True)
-                out[n] += [len(j[3]) for j in handed(helper(src, u, buf, T, topo), buf, k, T, topo)[0] if j[:2] == (src, u)][0]
-            else:
-                out[n] += [len(e) for calls in plan(src, buf, T, topo) for call in calls for us, to, e in call if us == [u]][0]
+    for src, (col, n) in landing(rank, T, topo).items():
+        for kind, items in writes(src, T, topo):
+            for u, to, eng, handed in items:
+                if peer(src, u, T, topo) == rank:
+                    out[n] += len(onward(to, kind + " " + u, T.cores[rank], topo) if handed else eng)
     return out
 
 
@@ -210,60 +176,37 @@ def rank_program(g, core, T, topo):
         return helper_program(g, core, T, topo)
     S, V, A, E, Y = T.sem, g.vector, g.scalar, g.tensor, g.sync
     COPY, RELU = ActivationFunctionType.Copy, ActivationFunctionType.Relu
-    BS = (0, 2, 1, 3)
-    mate = peer(rank, "M", 1, T, topo)
-    at, pieces, mspot = columns(rank, T, topo)
+    at, steps, moves = gathered(rank, T, topo)
 
     for q in range(2):
-        (Y, A)[q].dma_start(T.lst[16 * q:16 * q + 16, 0:32], T.snd[:, :]).then_inc(S.lst, 16)
-    Y.dma_start(T.xs[:, PAD:PAD + 4 * W], T.x[:, :]).then_inc(S.xin, 16)
-    wsem = {}
-    for j, (b0, b1) in enumerate(C["wload"]):
-        Y.dma_start(T.ws[:, 512 * b0:512 * b1], T.w[:, 512 * b0:512 * b1]).then_inc(S["win%d" % j], 16)
-        for b in range(b0, b1):
-            wsem[b] = S["win%d" % j]
+        Y.dma_start(T.lst[16 * q:16 * q + 16, 4:4 + 4 * N], T.snd[:, :]).then_inc(S.lst, 16)
+    for q, lo, hi in ((A, 0, 16), (Y, 16, 128)):
+        q.dma_start(T.xs[lo:hi, PAD:PAD + 4 * W], T.x[lo:hi, :]).then_inc(S.xin, 16)
+    Y.dma_start(T.ws[:], T.w[:, :]).then_inc(S.win, 16)
     Y.dma_start(T.pkl[:], T.pk[:, :]).then_inc(S.pkin, 16)
     Y.dma_start(T.vs[:], T.v[:, :]).then_inc(S.vin, 16)
 
     V.memset(T.xs[:, 0:PAD], 0.0).then_inc(S.pad, 1)
-    pads = 1
-    for k, step in enumerate(C["steps"]):
-        if len(step) < 2:
-            V.memset(T.gath[:, 4 * (pieces[k][2] - CAP):4 * pieces[k][2]], 0.0).then_inc(S.pad, 1)
-            pads += 1
     for b in range(4):
         V.memset(T["res%d" % b][:, W + CAP * rank:W + CAP * rank + CAP], 0.0).then_inc(S["fill%d" % b], 1)
     V.wait_ge(S.lst, 32)
-    wid = max(32, 4 * mspot + 4)
-    if mspot != mate:
-        V.tensor_copy(T.lst[0:32, 4 * mspot:4 * mspot + 4], T.lst[0:32, 4 * mate:4 * mate + 4]).then_inc(S.rep2, 1)
-        V.wait_ge(S.rep2, 1)
+    for to, frm in moves:
+        V.tensor_copy(T.lst[0:32, 4 * to:4 * to + 4], T.lst[0:32, 4 * frm:4 * frm + 4]).then_inc(S.moved, 1)
+    if moves:
+        V.wait_ge(S.moved, len(moves))
+    low, high = 4 * min(s[0] for s in steps + [(1, 1)]), 4 * max(s[1] for s in steps + [(N + 1, N + 1)])
     for q in range(1, 4):
-        V.tensor_copy(T.lst[32 * q:32 * q + 32, 0:wid], T.lst[0:32, 0:wid]).then_inc(S.rep0, 1)
-    V.wait_ge(S.rep0, 3)
+        V.tensor_copy(T.lst[32 * q:32 * q + 32, low:high], T.lst[0:32, low:high]).then_inc(S.spread, 1)
+    V.wait_ge(S.spread, 3)
     for t in (2, 0, 3, 1):
-        V.tensor_scalar(T["off%d" % t][:, 0:wid], T.lst[:, 0:wid], 4.0, float(PAD + t), AluOpType.mult,
+        V.tensor_scalar(T["off%d" % t][:, low:high], T.lst[:, low:high], 4.0, float(PAD + t), AluOpType.mult,
                         AluOpType.add).then_inc(S["off%d" % t], 1)
 
-    for q in (V, A):
-        q.wait_ge(S.pad, pads)
-        q.wait_ge(S.xin, 16)
-        for t in range(4):
-            q.wait_ge(S["off%d" % t], 1)
-
-    def quant_w(b):
-        V.wait_ge(wsem[b], 16)
-        V.quantize_mx(T.wq[:, 128 * b:128 * b + 128], T.wp[:, 128 * b:128 * b + 128],
-                      T.ws[:, 512 * b:512 * b + 512]).then_inc(S["wqd%d" % b], 1)
-
-    def gather(q, k, t):
-        for d0, d1, c in pieces[k][0]:
-            out = T.gath[:, 4 * c + t:4 * (c + CAP * (d1 - d0)):4]
-            src = T.xs[:, 0:PAD + 4 * W].indirect(T["off%d" % t][:, 4 * d0:4 * d1])
-            if q is V:
-                V.tensor_copy(out, src).then_inc(S["gat%d" % k], 1)
-            else:
-                A.activation(out, src, COPY).then_inc(S["gat%d" % k], 1)
+    def move(q, out, src, sem):
+        if q is V:
+            V.tensor_copy(out, src).then_inc(sem, 1)
+        else:
+            A.activation(out, src, COPY).then_inc(sem, 1)
 
     def keep(q, b, bank, skip, lo, n, done):
         src, out = T.ps[:, 512 * bank + skip:512 * bank + skip + n], T["res%d" % b][:, lo:lo + n]
@@ -273,19 +216,27 @@ def rank_program(g, core, T, topo):
             A.activation(out, src, RELU, scale=0.05).then_inc(S["%s%d" % (done, b)], 1)
 
     for q, words in ((V, C["V"]), (A, C["A"])):
+        q.wait_ge(S.pad, 1)
+        q.wait_ge(S.xin, 32)
         for word in words.split():
             op, n = word[0], [int(c) for c in word[1:]]
             if op == "g":
-                gather(q, n[0], n[1])
+                first, last, lo, hi = steps[n[0]]
+                q.wait_ge(S["off%d" % n[1]], 1)
+                move(q, T.gath[:, 4 * lo + n[1]:4 * hi:4],
+                     T.xs[:, 0:PAD + 4 * W].indirect(T["off%d" % n[1]][:, 4 * first:4 * last]), S["gat%d" % n[0]])
             elif op == "q":
-                runs, lo, hi = pieces[n[0]]
-                V.wait_ge(S["gat%d" % n[0]], 4 * len(runs))
+                first, last, lo, hi = steps[n[0]]
+                V.wait_ge(S["gat%d" % n[0]], 4)
                 V.quantize_mx(T.sq[:, lo:hi], T.sp[:, lo:hi], T.gath[:, 4 * lo:4 * hi]).then_inc(S["sqd%d" % n[0]], 1)
             elif op == "x":
                 lo, hi = 128 * n[0], 128 * n[1]
                 V.quantize_mx(T.cq[:, lo:hi], T.cp[:, lo:hi], T.xs[:, PAD + 4 * lo:PAD + 4 * hi]).then_inc(S.xqd, n[1] - n[0])
             elif op == "w":
-                quant_w(n[0])
+                b = n[0]
+                V.wait_ge(S.win, 16)
+                V.quantize_mx(T.wq[:, 128 * b:128 * b + 128], T.wp[:, 128 * b:128 * b + 128],
+                              T.ws[:, 512 * b:512 * b + 512]).then_inc(S["wqd%d" % b], 1)
             elif op == "k":
                 q.wait_ge(S["mo%d" % n[0]], 1)
                 keep(q, n[0], n[0], 0, 0, W, "ro")
@@ -297,131 +248,86 @@ def rank_program(g, core, T, topo):
                 V.quantize_mx(T.vq[:], T.vp[:], T.vs[:]).then_inc(S.vqd, 1)
 
     sent = 0
-    for k in range(len(C["steps"])):
-        g.wait_ge(S["sqd%d" % k], 1)
-        for buf, land in (("sq", "cq"), ("sp", "cp"))[::C["first"][k]]:
-            for call in plan(rank, buf, T, topo)[k]:
-                trs = []
-                for units, to, eng in call:
-                    a = view(T, buf, at[units[0]], CAP * len(units))
-                    if relayed(units[0], buf):
-                        trs.append(transfer(T, topo, to, eng, S["%s%d" % (buf, k)], a, a))
-                    else:
-                        colm, n = layout(T.rank_of(to), T, topo)[units[0]]
-                        trs.append(transfer(T, topo, to, eng, S["arr%d" % n], a, view(T, land, colm, CAP)))
-                    sent += len(eng)
-                g.remote_dma_fused(trs, local_sem=S.loc)
+    for i, (kind, items) in enumerate(writes(rank, T, topo)):
+        trs = []
+        for u, to, eng, handed in items:
+            g.wait_ge(S["sqd%d" % [u in step for step in C["steps"]].index(True)], 1)
+            a = view(T, kind, False, at[u])
+            if handed:
+                trs.append(transfer(topo, to, eng, S["hand%d" % i], a, a))
+            else:
+                col, n = landing(T.rank_of(to), T, topo)[rank]
+                trs.append(transfer(topo, to, eng, S["arr%d" % n], a, view(T, kind, True, col)))
+            sent += len(eng)
+        g.remote_dma_fused(trs, local_sem=S.loc)
     g.wait_ge(S.loc, sent)
 
     def product(b, bank, lo, hi, done):
         E.matmul_mx(T.ps[:, 512 * bank:512 * bank + hi - lo], T.wq[:, 128 * b:128 * b + 128], T.wp[:, 128 * b:128 * b + 128],
                     T.cq[:, lo:hi], T.cp[:, lo:hi], True, True).then_inc(S["%s%d" % (done, b)], 1)
 
-    lay = layout(rank, T, topo)
-    kept = {"fill": 1, "ro": 1}
-
-    def ready(q, b):
-        for k in kept:
-            q.wait_ge(S["%s%d" % (k, b)], kept[k])
-
-    def pick(q, b, lo, hi, done):
-        out = T.h[:, 4 * lo + b:4 * hi:4]
-        idx = T["res%d" % b][:, 0:W + N * CAP].indirect(T.pko[:, lo // 16:hi // 16])
-        if q is V:
-            V.tensor_copy(out, idx).then_inc(done, 1)
-        else:
-            A.activation(out, idx, COPY).then_inc(done, 1)
-
     E.wait_ge(S.xqd, 4)
     for b in [int(word[1]) for word in C["V"].split() if word[0] == "w"]:
         E.wait_ge(S["wqd%d" % b], 1)
         product(b, b, 0, W, "mo")
 
-    parts = C["parts"]
-    nr = len(C["runs"])
-    exp = expected(rank, T, topo)
+    lay, exp = landing(rank, T, topo), expected(rank, T, topo)
+    kept = {"fill": 1, "ro": 1}
     last_user = {0: "ro"}
-    for n, run in enumerate(C["runs"]):
-        if n == C["vq_at"]:
-            V.wait_ge(S.vin, 16)
-            V.quantize_mx(T.vq[:], T.vp[:], T.vs[:]).then_inc(S.vqd, 1)
+    for n in range(len(C["runs"])):
+        run = [s for s in range(N) if s in lay and lay[s][1] == n]
         E.wait_ge(S["arr%d" % n], exp[n])
-        lo = min(lay[u][0] for u in run)
-        hi = lo + CAP * len(run)
-        back = CAP if len(run) < 2 else 0
+        lo = lay[run[0]][0] - (CAP if len(run) < 2 else 0)
+        hi = lay[run[-1]][0] + CAP
         segs = []
-        for u in sorted(run, key=lambda u: lay[u][0]):
-            s = peer(rank, u, -1, T, topo)
+        for s in run:
             if segs and segs[-1][1] + segs[-1][2] == W + CAP * s:
                 segs[-1][2] += CAP
             else:
-                segs.append([lay[u][0] - lo + back, W + CAP * s, CAP])
+                segs.append([lay[s][0] - lo, W + CAP * s, CAP])
         made, done = "m" + "abcd"[n], "r" + "abcd"[n]
         kept[done] = len(segs)
         half = 4 * ((n + 1) % 2)
-        for b in BS:
-            q = V if b in C.get("fkeep", ((0, 1),) * 4)[n] else A
+        for b in (0, 2, 1, 3):
+            q = V if b in C["fkeep"][n] else A
             if half in last_user:
                 E.wait_ge(S["%s%d" % (last_user[half], b)], kept[last_user[half]])
-            product(b, half + b, lo - back, hi, made)
+            product(b, half + b, lo, hi, made)
             q.wait_ge(S["%s%d" % (made, b)], 1)
             for skip, to, cnt in segs:
                 keep(q, b, half + b, skip, to, cnt, done)
-        for b in BS:
-            if n == nr - 1:
-                q = V if b < 2 else A
-                if b in (0, 2):
-                    q.wait_ge(S.pkd, 1)
-                ready(q, b)
-                pick(q, b, 0, parts[1], S.hg0)
         last_user[half] = done
 
-    np_ = len(parts) - 1
     E.wait_ge(S.vqd, 1)
-    aready = [False]
-    free = 4 * (nr % 2 == 0)
-
-    def copy_out(n, q):
-        lo, hi = parts[n], parts[n + 1]
-        src, out = T.ps[:, 512 * (free + n):512 * (free + n) + hi - lo], T.ys[:, lo:hi]
-        q.wait_ge(S["my%d" % n], 1)
-        if q is A:
-            A.activation(out, src, COPY).then_inc(S["cy%d" % n], 1)
-        else:
-            V.tensor_copy(out, src).then_inc(S["cy%d" % n], 1)
-        Y.wait_ge(S["cy%d" % n], 1)
-        Y.dma_start(T.y[:, lo:hi], T.ys[:, lo:hi]).then_inc(S["out%d" % n], 16)
-
-    def quant_h(n, cnt):
-        lo, hi = parts[n], parts[n + 1]
-        V.wait_ge(S["hg%d" % n], cnt)
-        V.quantize_mx(T.hq[:, lo:hi], T.hp[:, lo:hi], T.h[:, 4 * lo:4 * hi]).then_inc(S["hq%d" % n], 1)
-        E.wait_ge(S["hq%d" % n], 1)
-        E.wait_ge(S["%s%d" % (last_user[free], n)], kept[last_user[free]])
-        E.matmul_mx(T.ps[:, 512 * (free + n):512 * (free + n) + hi - lo], T.vq[:], T.vp[:], T.hq[:, lo:hi], T.hp[:, lo:hi],
-                    True, True).then_inc(S["my%d" % n], 1)
-
-    cnt = 4
-    Ms = C["M"] if isinstance(C["M"], tuple) else (C["M"],)
-    for n in range(1, np_):
-        lo, hi, M = parts[n], parts[n + 1], Ms[n - 1]
-        s = S["hg%d" % n]
-        pick(V, 0, lo, hi, s)
-        quant_h(n - 1, cnt)
-        cnt = 3
-        if M > lo:
-            pick(V, 1, lo, M, s)
-            cnt += 1
-        pick(A, 2, lo, hi, s)
-        pick(A, 3, lo, hi, s)
-        if M < hi:
-            if not aready[0]:
-                ready(A, 1)
-                aready[0] = True
-            pick(A, 1, M, hi, s)
-            cnt += 1
-        copy_out(n - 1, A)
-    quant_h(np_ - 1, cnt)
-    copy_out(np_ - 1, V)
-    for n in range(np_):
+    free = 4 - half
+    picks = [w for q in ("TV", "TA") for w in C[q] if w[0] == "p"]
+    for q, words in ((V, C["TV"]), (A, C["TA"])):
+        q.wait_ge(S.pkd, 1)
+        for w in words:
+            if w[0] == "p":
+                b, lo, hi = w[1:]
+                for k in kept:
+                    q.wait_ge(S["%s%d" % (k, b)], kept[k])
+                move(q, T.h[:, 4 * lo + b:4 * hi:4], T["res%d" % b][:, 0:W + N * CAP].indirect(T.pko[:, lo // 16:hi // 16]),
+                     S["hg%d" % picks.index(w)])
+                continue
+            n = w[1]
+            lo, hi = PART * n, PART * n + PART
+            bank = T.ps[:, 512 * (free + n):512 * (free + n) + PART]
+            if w[0] == "q":
+                for i, c in enumerate(picks):
+                    if c[2] < hi and c[3] > lo:
+                        V.wait_ge(S["hg%d" % i], 1)
+                V.quantize_mx(T.hq[:, lo:hi], T.hp[:, lo:hi], T.h[:, 4 * lo:4 * hi]).then_inc(S["hq%d" % n], 1)
+                E.wait_ge(S["hq%d" % n], 1)
+                E.wait_ge(S["%s%d" % (last_user[free], n)], kept[last_user[free]])
+                E.matmul_mx(bank, T.vq[:], T.vp[:], T.hq[:, lo:hi], T.hp[:, lo:hi], True, True).then_inc(S["my%d" % n], 1)
+            else:
+                q.wait_ge(S["my%d" % n], 1)
+                move(q, T.ys[:, lo:hi], bank, S["cy%d" % n])
+    for n in range(PICKS // PART):
+        q = A if n == PICKS // PART - 1 else Y
+        q.wait_ge(S["cy%d" % n], 1)
+        q.dma_start(T.y[:, PART * n:PART * n + PART], T.ys[:, PART * n:PART * n + PART]).then_inc(S["out%d" % n], 16)
+    for n in range(PICKS // PART):
         Y.wait_ge(S["out%d" % n], 16)

from concourse.bass import DstId, RemoteDMATransfer
from concourse.mybir import dt, AluOpType, ActivationFunctionType

N, W, CAP, PICKS = 8, 512, 64, 512
PAD = 16
PART = 128
CODES, BYTE = "float8_e4m3fn_x4", "uint8"
C = dict(
    steps=(("a", "c0"), ("b0", "b1", "m"), ("e", "c1")),
    calls=("q a c0", "p a c0", "q b0 b1 m", "p e c1", "p b0 b1 m", "q e", "q c1"),
    road={"q c0": 0, "p c0": 1, "p c1": 0}, halves={0: (0, 4, 1), 1: (4, 8, 1)}, neng=8,
    runs=(("a", "m"), ("b0", "b1"), ("e",), ("c0", "c1")),
    V="g00 g01 q0 g10 g11 x01 q1 x14 w2 q2 w3 w0 w1 p v k0", A="g02 g03 g12 g13 g20 g21 g22 g23 k2 k3 k1",
    fkeep=((0, 1, 2), (0, 1), (0, 1), (0, 1)),
    TV=(("p", 0, 0, 256), ("p", 1, 0, 416), ("p", 3, 192, 384), ("q", 0), ("q", 1), ("p", 1, 416, 512), ("q", 2), ("q", 3),
        ("c", 3)),
    TA=(("p", 2, 0, 512), ("p", 3, 0, 192), ("p", 0, 256, 512), ("p", 3, 384, 512), ("c", 0), ("c", 1), ("c", 2)),
)
SCRATCH = {
    "lst": ("sbuf", [128, 4 * (N + 2)], "int32"),
    "pkl": ("sbuf", [128, 32], "int32"),
    "pko": ("sbuf", [128, 32], "uint16"),
    "xs": ("sbuf", [128, PAD + 4 * W], "bfloat16"),
    "ws": ("sbuf", [128, 2048], "bfloat16"),
    "vs": ("sbuf", [128, 512], "bfloat16"),
    "gath": ("sbuf", [128, 4 * 7 * CAP], "bfloat16"),
    "sq": ("sbuf", [128, 7 * CAP], CODES),
    "sp": ("sbuf", [128, 7 * CAP], BYTE),
    "cq": ("sbuf", [128, W + 7 * CAP], CODES),
    "cp": ("sbuf", [128, W + 7 * CAP], BYTE),
    "wq": ("sbuf", [128, 512], CODES),
    "wp": ("sbuf", [128, 512], BYTE),
    "vq": ("sbuf", [128, 128], CODES),
    "vp": ("sbuf", [128, 128], BYTE),
    "h": ("sbuf", [128, 4 * PICKS], "bfloat16"),
    "hq": ("sbuf", [128, PICKS], CODES),
    "hp": ("sbuf", [128, PICKS], BYTE),
    "ys": ("sbuf", [128, PICKS], "float32"),
    "ps": ("psum", [128, 4096], "float32"),
}
for _t in range(4):
    SCRATCH["off%d" % _t] = ("sbuf", [128, 4 * (N + 2)], "uint16")
    SCRATCH["res%d" % _t] = ("sbuf", [128, W + N * CAP], "bfloat16")
SEMAPHORES = (["lst", "moved", "spread", "xin", "win", "pkin", "vin", "pad", "xqd", "vqd", "pkd", "loc"]
              + [k + "%d" % i for k in ("hg", "hand") for i in range(10)]
              + [k + "%d" % i for k in ("wqd", "off", "gat", "sqd", "fill", "mo", "ro", "hq", "my", "cy", "out",
                                        "arr", "ma", "mb", "mc", "md", "ra", "rb", "rc", "rd") for i in range(4)])


def groups_of(T, topo):
    out = {}
    for r, c in enumerate(T.cores):
        out.setdefault(topo.chip(c), []).append(r)
    return [out[k] for k in sorted(out, key=lambda k: out[k][0])]


def peer(rank, name, T, topo):
    groups = groups_of(T, topo)
    m = [rank in q for q in groups].index(True)
    j = groups[m].index(rank)
    way = 2 * j - 1
    if name == "m":
        return groups[m][1 - j]
    if name[0] == "c":
        plane = [q for q in groups if topo.same_plane(topo.chip(T.cores[q[0]]), topo.chip(T.cores[rank]))][0]
        return plane[j ^ int(name[1])]
    if name[0] == "b":
        return groups[(m - way) % len(groups)][int(name[1])]
    return groups[(m + way) % len(groups)][1 - j if name == "a" else j]


def gathered(rank, T, topo):
    at, steps, moves, col = {}, [], [], 0
    for step in C["steps"]:
        place = {u: 1 + peer(rank, u, T, topo) for u in step}
        beside = [min(place[u] for u in step[:-1]) - 1, max(place[u] for u in step[:-1]) + 1]
        if place[step[-1]] not in beside:
            free = [i for i in beside if i in (0, 1 + rank, N + 1)][0]
            moves.append((free, place[step[-1]]))
            place[step[-1]] = free
        low = min(place.values())
        for u in step:
            at[u] = col + CAP * (place[u] - low)
        steps.append((low, low + len(step), col, col + CAP * len(step)))
        col += CAP * len(step)
    return at, steps, moves


def landing(dst, T, topo):
    out, col = {}, W
    for n, run in enumerate(C["runs"]):
        for s in range(N):
            if dst in [peer(s, u, T, topo) for u in run]:
                out[s] = (col, n)
                col += CAP
    return out


def helper(src, which, T, topo):
    me = T.cores[src]
    j = [q.index(src) for q in groups_of(T, topo) if src in q][0]
    return [c for c in topo.cores_of(me) if topo.die(c) != topo.die(me)][2 * which + j]


def writes(src, T, topo):
    core, out = T.cores[src], []
    away = topo.engines(core, T.cores[peer(src, "a", T, topo)])
    for call in C["calls"]:
        kind, names = call.split()[0], call.split()[1:]
        road = {u: C["road"].get(kind + " " + u) for u in names}
        to = {u: T.cores[peer(src, u, T, topo)] if road[u] is None else helper(src, road[u], T, topo) for u in names}
        far = [u for u in names if topo.chip(to[u]) != topo.chip(core)]
        items = []
        for u in names:
            like = far if u in far else [v for v in names if v not in far]
            eng = away if u in far else [e for e in topo.engines(core, to[u]) if e not in away][::8 // C["neng"]]
            if u in far and len(out) in C["halves"]:
                eng = eng[C["halves"][len(out)][0]:C["halves"][len(out)][1]:C["halves"][len(out)][2]]
            share = 1
            while 2 * share * len(like) <= len(eng):
                share *= 2
            k = like.index(u)
            items.append((u, to[u], eng[k * share:(k + 1) * share], road[u] is not None))
        out.append((kind, items))
    return out


def view(T, kind, landed, lo):
    if kind == "q":
        return T["cq" if landed else "sq"][:, lo:lo + CAP].bitcast(dt.uint8)
    return T["cp" if landed else "sp"][:, lo:lo + CAP]


def transfer(topo, to, engines, sem, a, b):
    rid, pid, _ = topo.addr(to)
    return RemoteDMATransfer(dst_ids=[DstId(rid=rid, pnc=pid)], dma_engine_mask=sum(1 << e for e in engines),
                             remote_sem=sem, src=a, dst=b)


def onward(core, job, to, topo):
    jobs = [j for j in C["road"] if C["road"][j] == C["road"][job]]
    return topo.engines(core, to)[jobs.index(job)::2]


def helper_program(g, core, T, topo):
    total = 0
    for src in range(N):
        for i, (kind, items) in enumerate(writes(src, T, topo)):
            for u, to, eng, handed in items:
                if handed and to == core:
                    dst = peer(src, u, T, topo)
                    col, n = landing(dst, T, topo)[src]
                    away = onward(core, kind + " " + u, T.cores[dst], topo)
                    g.wait_ge(T.sem["hand%d" % i], len(eng))
                    g.remote_dma_fused([transfer(topo, T.cores[dst], away, T.sem["arr%d" % n],
                                                 view(T, kind, False, gathered(src, T, topo)[0][u]), view(T, kind, True, col))],
                                       local_sem=T.sem.loc)
                    total += len(away)
    if total:
        g.wait_ge(T.sem.loc, total)


def expected(rank, T, topo):
    out = [0] * len(C["runs"])
    for src, (col, n) in landing(rank, T, topo).items():
        for kind, items in writes(src, T, topo):
            for u, to, eng, handed in items:
                if peer(src, u, T, topo) == rank:
                    out[n] += len(onward(to, kind + " " + u, T.cores[rank], topo) if handed else eng)
    return out


def rank_program(g, core, T, topo):
    rank = T.rank_of(core)
    if rank is None:
        return helper_program(g, core, T, topo)
    S, V, A, E, Y = T.sem, g.vector, g.scalar, g.tensor, g.sync
    COPY, RELU = ActivationFunctionType.Copy, ActivationFunctionType.Relu
    at, steps, moves = gathered(rank, T, topo)

    for q in range(2):
        Y.dma_start(T.lst[16 * q:16 * q + 16, 4:4 + 4 * N], T.snd[:, :]).then_inc(S.lst, 16)
    for q, lo, hi in ((A, 0, 16), (Y, 16, 128)):
        q.dma_start(T.xs[lo:hi, PAD:PAD + 4 * W], T.x[lo:hi, :]).then_inc(S.xin, 16)
    Y.dma_start(T.ws[:], T.w[:, :]).then_inc(S.win, 16)
    Y.dma_start(T.pkl[:], T.pk[:, :]).then_inc(S.pkin, 16)
    Y.dma_start(T.vs[:], T.v[:, :]).then_inc(S.vin, 16)

    V.memset(T.xs[:, 0:PAD], 0.0).then_inc(S.pad, 1)
    for b in range(4):
        V.memset(T["res%d" % b][:, W + CAP * rank:W + CAP * rank + CAP], 0.0).then_inc(S["fill%d" % b], 1)
    V.wait_ge(S.lst, 32)
    for to, frm in moves:
        V.tensor_copy(T.lst[0:32, 4 * to:4 * to + 4], T.lst[0:32, 4 * frm:4 * frm + 4]).then_inc(S.moved, 1)
    if moves:
        V.wait_ge(S.moved, len(moves))
    low, high = 4 * min(s[0] for s in steps + [(1, 1)]), 4 * max(s[1] for s in steps + [(N + 1, N + 1)])
    for q in range(1, 4):
        V.tensor_copy(T.lst[32 * q:32 * q + 32, low:high], T.lst[0:32, low:high]).then_inc(S.spread, 1)
    V.wait_ge(S.spread, 3)
    for t in (2, 0, 3, 1):
        V.tensor_scalar(T["off%d" % t][:, low:high], T.lst[:, low:high], 4.0, float(PAD + t), AluOpType.mult,
                        AluOpType.add).then_inc(S["off%d" % t], 1)

    def move(q, out, src, sem):
        if q is V:
            V.tensor_copy(out, src).then_inc(sem, 1)
        else:
            A.activation(out, src, COPY).then_inc(sem, 1)

    def keep(q, b, bank, skip, lo, n, done):
        src, out = T.ps[:, 512 * bank + skip:512 * bank + skip + n], T["res%d" % b][:, lo:lo + n]
        if q is V:
            V.tensor_scalar(out, src, 0.0, 0.05, AluOpType.max, AluOpType.mult).then_inc(S["%s%d" % (done, b)], 1)
        else:
            A.activation(out, src, RELU, scale=0.05).then_inc(S["%s%d" % (done, b)], 1)

    for q, words in ((V, C["V"]), (A, C["A"])):
        q.wait_ge(S.pad, 1)
        q.wait_ge(S.xin, 32)
        for word in words.split():
            op, n = word[0], [int(c) for c in word[1:]]
            if op == "g":
                first, last, lo, hi = steps[n[0]]
                q.wait_ge(S["off%d" % n[1]], 1)
                move(q, T.gath[:, 4 * lo + n[1]:4 * hi:4],
                     T.xs[:, 0:PAD + 4 * W].indirect(T["off%d" % n[1]][:, 4 * first:4 * last]), S["gat%d" % n[0]])
            elif op == "q":
                first, last, lo, hi = steps[n[0]]
                V.wait_ge(S["gat%d" % n[0]], 4)
                V.quantize_mx(T.sq[:, lo:hi], T.sp[:, lo:hi], T.gath[:, 4 * lo:4 * hi]).then_inc(S["sqd%d" % n[0]], 1)
            elif op == "x":
                lo, hi = 128 * n[0], 128 * n[1]
                V.quantize_mx(T.cq[:, lo:hi], T.cp[:, lo:hi], T.xs[:, PAD + 4 * lo:PAD + 4 * hi]).then_inc(S.xqd, n[1] - n[0])
            elif op == "w":
                b = n[0]
                V.wait_ge(S.win, 16)
                V.quantize_mx(T.wq[:, 128 * b:128 * b + 128], T.wp[:, 128 * b:128 * b + 128],
                              T.ws[:, 512 * b:512 * b + 512]).then_inc(S["wqd%d" % b], 1)
            elif op == "k":
                q.wait_ge(S["mo%d" % n[0]], 1)
                keep(q, n[0], n[0], 0, 0, W, "ro")
            elif op == "p":
                V.wait_ge(S.pkin, 16)
                V.tensor_copy(T.pko[:], T.pkl[:]).then_inc(S.pkd, 1)
            elif op == "v":
                V.wait_ge(S.vin, 16)
                V.quantize_mx(T.vq[:], T.vp[:], T.vs[:]).then_inc(S.vqd, 1)

    sent = 0
    for i, (kind, items) in enumerate(writes(rank, T, topo)):
        trs = []
        for u, to, eng, handed in items:
            g.wait_ge(S["sqd%d" % [u in step for step in C["steps"]].index(True)], 1)
            a = view(T, kind, False, at[u])
            if handed:
                trs.append(transfer(topo, to, eng, S["hand%d" % i], a, a))
            else:
                col, n = landing(T.rank_of(to), T, topo)[rank]
                trs.append(transfer(topo, to, eng, S["arr%d" % n], a, view(T, kind, True, col)))
            sent += len(eng)
        g.remote_dma_fused(trs, local_sem=S.loc)
    g.wait_ge(S.loc, sent)

    def product(b, bank, lo, hi, done):
        E.matmul_mx(T.ps[:, 512 * bank:512 * bank + hi - lo], T.wq[:, 128 * b:128 * b + 128], T.wp[:, 128 * b:128 * b + 128],
                    T.cq[:, lo:hi], T.cp[:, lo:hi], True, True).then_inc(S["%s%d" % (done, b)], 1)

    E.wait_ge(S.xqd, 4)
    for b in [int(word[1]) for word in C["V"].split() if word[0] == "w"]:
        E.wait_ge(S["wqd%d" % b], 1)
        product(b, b, 0, W, "mo")

    lay, exp = landing(rank, T, topo), expected(rank, T, topo)
    kept = {"fill": 1, "ro": 1}
    last_user = {0: "ro"}
    for n in range(len(C["runs"])):
        run = [s for s in range(N) if s in lay and lay[s][1] == n]
        E.wait_ge(S["arr%d" % n], exp[n])
        lo = lay[run[0]][0] - (CAP if len(run) < 2 else 0)
        hi = lay[run[-1]][0] + CAP
        segs = []
        for s in run:
            if segs and segs[-1][1] + segs[-1][2] == W + CAP * s:
                segs[-1][2] += CAP
            else:
                segs.append([lay[s][0] - lo, W + CAP * s, CAP])
        made, done = "m" + "abcd"[n], "r" + "abcd"[n]
        kept[done] = len(segs)
        half = 4 * ((n + 1) % 2)
        for b in (0, 2, 1, 3):
            q = V if b in C["fkeep"][n] else A
            if half in last_user:
                E.wait_ge(S["%s%d" % (last_user[half], b)], kept[last_user[half]])
            product(b, half + b, lo, hi, made)
            q.wait_ge(S["%s%d" % (made, b)], 1)
            for skip, to, cnt in segs:
                keep(q, b, half + b, skip, to, cnt, done)
        last_user[half] = done

    E.wait_ge(S.vqd, 1)
    free = 4 - half
    picks = [w for q in ("TV", "TA") for w in C[q] if w[0] == "p"]
    for q, words in ((V, C["TV"]), (A, C["TA"])):
        q.wait_ge(S.pkd, 1)
        for w in words:
            if w[0] == "p":
                b, lo, hi = w[1:]
                for k in kept:
                    q.wait_ge(S["%s%d" % (k, b)], kept[k])
                move(q, T.h[:, 4 * lo + b:4 * hi:4], T["res%d" % b][:, 0:W + N * CAP].indirect(T.pko[:, lo // 16:hi // 16]),
                     S["hg%d" % picks.index(w)])
                continue
            n = w[1]
            lo, hi = PART * n, PART * n + PART
            bank = T.ps[:, 512 * (free + n):512 * (free + n) + PART]
            if w[0] == "q":
                for i, c in enumerate(picks):
                    if c[2] < hi and c[3] > lo:
                        V.wait_ge(S["hg%d" % i], 1)
                V.quantize_mx(T.hq[:, lo:hi], T.hp[:, lo:hi], T.h[:, 4 * lo:4 * hi]).then_inc(S["hq%d" % n], 1)
                E.wait_ge(S["hq%d" % n], 1)
                E.wait_ge(S["%s%d" % (last_user[free], n)], kept[last_user[free]])
                E.matmul_mx(bank, T.vq[:], T.vp[:], T.hq[:, lo:hi], T.hp[:, lo:hi], True, True).then_inc(S["my%d" % n], 1)
            else:
                q.wait_ge(S["my%d" % n], 1)
                move(q, T.ys[:, lo:hi], bank, S["cy%d" % n])
    for n in range(PICKS // PART):
        q = A if n == PICKS // PART - 1 else Y
        q.wait_ge(S["cy%d" % n], 1)
        q.dma_start(T.y[:, PART * n:PART * n + PART], T.ys[:, PART * n:PART * n + PART]).then_inc(S["out%d" % n], 16)
    for n in range(PICKS // PART):
        Y.wait_ge(S["out%d" % n], 16)
